import numpy as np, ml_dtypes
CORES = [3,5,19,21,35,37,51,53,67,69]
N = 10
NP, NBK, TK, CAP = 5, 4, 128, 6
DEST = [[5,8,5,5],[9,9,7,8],[8,6,5,9],[6,9,8,8],[6,5,5,9]]
def setup_inputs(rng):
    return {"x": rng.standard_normal((N, 128, NBK * TK), dtype=np.float32).astype(ml_dtypes.bfloat16), "w": (rng.standard_normal((N, 128, 128), dtype=np.float32) / 8).astype(ml_dtypes.bfloat16)}
def setup_inputs_big(rng):
    d = setup_inputs(rng)
    for k in ("x", "w"): d[k] = (d[k].astype(np.float32) * 1024.0).astype(d[k].dtype)
    return d
def setup_inputs_small(rng):
    d = setup_inputs(rng)
    for k in ("x", "w"): d[k] = (d[k].astype(np.float32) * (1 / 1024.0)).astype(d[k].dtype)
    return d
def setup_inputs_apart(rng):
    d = setup_inputs(rng)
    f = (10.0 ** rng.permutation(np.linspace(-1.5, 1.5, N))).astype(np.float32).reshape(N, 1, 1)
    for k in ("x", "w"): d[k] = (d[k].astype(np.float32) * f).astype(d[k].dtype)
    return d
def reference(x, w):
    X, W = x.astype(np.float64), w.astype(np.float64)
    y = np.full((N, 128, CAP * TK), np.nan); n = [0] * N
    for p in range(NP):
        for c in range(NBK):
            q = DEST[p][c]
            y[q][:, TK * n[q]:TK * n[q] + TK] = W[q].T @ np.maximum(W[p].T @ X[p][:, TK * c:TK * c + TK], 0.0)
            n[q] += 1
    return {"y": y.astype(ml_dtypes.bfloat16 if x.dtype != np.float64 else np.float64)}

@@ -1,0 +1,131 @@
+from concourse.mybir import dt, AluOpType
+
+NP, NBK, TK, CAP = 5, 4, 128, 6
+
+SCRATCH = {
+    "wsb": ("sbuf", [128, TK], "bfloat16"),
+    "xsb": ("sbuf", [128, NBK * TK], "bfloat16"),
+    "zero": ("sbuf", [128, NBK * TK], "float32"),
+    "h": ("sbuf", [128, NBK * TK], "bfloat16"),
+    "land": ("sbuf", [128, CAP * TK], "bfloat16"),
+    "res": ("sbuf", [128, CAP * TK], "bfloat16"),
+}
+for _i in range(NP):
+    SCRATCH["ps%d" % _i] = ("psum", [128, 512], "float32")
+
+SEMAPHORES = (["ldw", "zr", "sent"]
+              + ["ldx%d" % i for i in range(NBK)]
+              + ["mm%d" % i for i in range(NP)]
+              + ["ew%d" % i for i in range(NP)]
+              + ["arr%d" % i for i in range(NP)]
+              + ["st%d" % i for i in range(NP)])
+
+
+def _runs(cs):
+    out = []
+    for c in cs:
+        if out and out[-1][0] + out[-1][1] == c:
+            out[-1][1] += 1
+        else:
+            out.append([c, 1])
+    return [(a, n) for a, n in out]
+
+
+def _plan(dest):
+    sends = []
+    for p in range(len(dest)):
+        byq = {}
+        for c, q in enumerate(dest[p]):
+            byq.setdefault(q, []).append(c)
+        order = sorted(byq, key=lambda q: (-len(byq[q]), (q + p) % len(dest)))
+        lst, src, when = [], 0, 0.0
+        for q in order:
+            n = len(byq[q])
+            when += 1.0 + 0.3 * n
+            dst = sum(1 for pp in range(p) for qq in dest[pp] if qq == q)
+            lst.append({"p": p, "q": q, "cs": byq[q], "src": src, "dst": dst, "n": n, "when": when})
+            src += n
+        sends.append(lst)
+    return sends
+
+
+def _mask_of(core, dsts, topo):
+    m = -1
+    for d in dsts:
+        m &= topo.mask(core, d)
+    return m
+
+
+def _sender(g, core, T, topo, p, mine):
+    S = T.sem
+    hw = [g.sync, g.scalar]
+    g.sync.dma_start(T.wsb[:], T.w[:]).then_inc(S.ldw, 16)
+    first = _runs(mine[0]["cs"])
+    rest = _runs(sorted(c for s in mine[1:] for c in s["cs"]))
+    sem_of_block = {}
+    for i, (a, n) in enumerate(first + rest):
+        hw[(i + 1) % 2].dma_start(T.xsb[:, a * TK:(a + n) * TK], T.x[:, a * TK:(a + n) * TK]).then_inc(S["ldx%d" % i], 16)
+        for c in range(a, a + n):
+            sem_of_block[c] = i
+    widest = max(s["n"] for s in mine) * TK
+    g.vector.memset(T.zero[:, 0:widest], 0.0).then_inc(S.zr, 1)
+    g.vector.wait_ge(S.zr, 1)
+    g.tensor.wait_ge(S.ldw, 16)
+    seen = set()
+    mask = _mask_of(core, [T.cores[s["q"]] for s in mine], topo)
+    eng = bin(mask).count("1")
+    for k, s in enumerate(mine):
+        ps = T["ps%d" % k]
+        runs = _runs(s["cs"])
+        at = 0
+        for a, n in runs:
+            for c in range(a, a + n):
+                i = sem_of_block[c]
+                if i not in seen:
+                    seen.add(i)
+                    g.tensor.wait_ge(S["ldx%d" % i], 16)
+            g.tensor.matmul(ps[:, at * TK:(at + n) * TK], T.wsb[:], T.xsb[:, a * TK:(a + n) * TK],
+                            start=True, stop=True).then_inc(S["mm%d" % k], 1)
+            at += n
+        wd = s["n"] * TK
+        hcols = T.h[:, s["src"] * TK:s["src"] * TK + wd]
+        g.vector.wait_ge(S["mm%d" % k], len(runs))
+        g.vector.tensor_tensor(out=hcols, in0=ps[:, 0:wd], in1=T.zero[:, 0:wd], op=AluOpType.max).then_inc(S["ew%d" % k], 1)
+        dst = T.cores[s["q"]]
+        assert topo.may_write(core, dst)
+        rid, pid, _ = topo.addr(dst)
+        g.wait_ge(S["ew%d" % k], 1)
+        g.remote_dma(T.land[:, s["dst"] * TK:s["dst"] * TK + wd], hcols, S["arr%d" % p], S.sent, pid, rid, mask)
+    g.wait_ge(S.sent, eng * len(mine))
+
+
+def _receiver(g, core, T, topo, q, sends):
+    S = T.sem
+    hw = [g.scalar, g.sync]
+    g.sync.dma_start(T.wsb[:], T.w[:]).then_inc(S.ldw, 16)
+    g.tensor.wait_ge(S.ldw, 16)
+    mine = sorted((s for lst in sends for s in lst if s["q"] == q), key=lambda s: (s["when"], s["p"]))
+    for k, s in enumerate(mine):
+        src = T.cores[s["p"]]
+        eng = bin(_mask_of(src, [T.cores[t["q"]] for t in sends[s["p"]]], topo)).count("1")
+        lo, hi = s["dst"] * TK, (s["dst"] + s["n"]) * TK
+        ps = T["ps%d" % k]
+        g.tensor.wait_ge(S["arr%d" % s["p"]], eng)
+        g.tensor.matmul(ps[:, 0:hi - lo], T.wsb[:], T.land[:, lo:hi], start=True, stop=True).then_inc(S["mm%d" % k], 1)
+        g.vector.wait_ge(S["mm%d" % k], 1)
+        g.vector.tensor_copy(out=T.res[:, lo:hi], in_=ps[:, 0:hi - lo]).then_inc(S["ew%d" % k], 1)
+        hw[k % 2].wait_ge(S["ew%d" % k], 1)
+        hw[k % 2].dma_start(T.y[:, lo:hi], T.res[:, lo:hi]).then_inc(S["st%d" % k], 16)
+    for k in range(len(mine)):
+        hw[k % 2].wait_ge(S["st%d" % k], 16)
+
+
+def rank_program(g, core, T, topo):
+    rank = T.rank_of(core)
+    if rank is None:
+        return
+    sends = _plan(T.tables["DEST"])
+    if rank < len(sends):
+        _sender(g, core, T, topo, rank, sends[rank])
+    else:
+        _receiver(g, core, T, topo, rank, sends)

@@ -1,24 +1,28 @@
 from concourse.mybir import dt, AluOpType
+from concourse.bass import DstId, RemoteDMATransfer
 
 NP, NBK, TK, CAP = 5, 4, 128, 6
 
 SCRATCH = {
-    "wsb": ("sbuf", [128, TK], "bfloat16"),
+    "wx": ("sbuf", [128, 2 * TK], "bfloat16"),
     "xsb": ("sbuf", [128, NBK * TK], "bfloat16"),
     "zero": ("sbuf", [128, NBK * TK], "float32"),
     "h": ("sbuf", [128, NBK * TK], "bfloat16"),
     "land": ("sbuf", [128, CAP * TK], "bfloat16"),
+    "rl": ("sbuf", [128, NP * 2 * TK], "bfloat16"),
     "res": ("sbuf", [128, CAP * TK], "bfloat16"),
 }
-for _i in range(NP):
+for _i in range(CAP):
     SCRATCH["ps%d" % _i] = ("psum", [128, 512], "float32")
 
 SEMAPHORES = (["ldw", "zr", "sent"]
               + ["ldx%d" % i for i in range(NBK)]
-              + ["mm%d" % i for i in range(NP)]
-              + ["ew%d" % i for i in range(NP)]
-              + ["arr%d" % i for i in range(NP)]
-              + ["st%d" % i for i in range(NP)])
+              + ["mm%d" % i for i in range(CAP)]
+              + ["ew%d" % i for i in range(CAP)]
+              + ["rm%d" % i for i in range(CAP)]
+              + ["re%d" % i for i in range(CAP)]
+              + ["arr%d" % i for i in range(CAP)]
+              + ["st%d" % i for i in range(CAP)])
 
 
 def _runs(cs):
@@ -31,40 +35,104 @@ def _runs(cs):
     return [(a, n) for a, n in out]
 
 
-def _plan(dest):
-    sends = []
-    for p in range(len(dest)):
-        byq = {}
-        for c, q in enumerate(dest[p]):
-            byq.setdefault(q, []).append(c)
-        order = sorted(byq, key=lambda q: (-len(byq[q]), (q + p) % len(dest)))
-        lst, src, when = [], 0, 0.0
-        for q in order:
-            n = len(byq[q])
-            when += 1.0 + 0.3 * n
-            dst = sum(1 for pp in range(p) for qq in dest[pp] if qq == q)
-            lst.append({"p": p, "q": q, "cs": byq[q], "src": src, "dst": dst, "n": n, "when": when})
-            src += n
-        sends.append(lst)
-    return sends
+def _perms(lst):
+    if len(lst) <= 1:
+        return [list(lst)]
+    return [[lst[i]] + r for i in range(len(lst)) for r in _perms(lst[:i] + lst[i + 1:])]
 
 
-def _mask_of(core, dsts, topo):
-    m = -1
-    for d in dsts:
-        m &= topo.mask(core, d)
-    return m
+def _pieces(dest, p):
+    byq = {}
+    for c, q in enumerate(dest[p]):
+        byq.setdefault(q, []).append(c)
+    out = []
+    for q in sorted(byq):
+        cs = byq[q]
+        at = sum(1 for pp in range(p) for qq in dest[pp] if qq == q)
+        for part in ([cs] if len(cs) < 3 else [cs[:1], cs[1:]]):
+            out.append({"p": p, "q": q, "cs": part, "n": len(part), "dst": at})
+            at += len(part)
+    return out
+
+
+def _dur(n):
+    return 1.0 + 0.3 * n
+
+
+def _cost(orders, cores, topo):
+    ev, c, load = [], 0.0, {}
+    for lst in orders:
+        t = 0.0
+        c += 100 * (lst[0]["n"] - 1) + 100 * (lst[-1]["n"] - 1)
+        for k, s in enumerate(lst):
+            d = _dur(s["n"]) * (2 if k == 0 else 1)
+            ev.append((t, t + d, s))
+            t += d
+            sc, dc = cores[s["p"]], cores[s["q"]]
+            if topo.chip(sc) != topo.chip(dc):
+                port = (topo.chip(dc), topo.die(sc))
+                load[port] = load.get(port, 0) + s["n"] + (1 if k == 0 else 0)
+    c += 10 * max(load.values())
+    for i, (a0, a1, a) in enumerate(ev):
+        for b0, b1, b in ev[:i]:
+            if a["p"] == b["p"]:
+                continue
+            sa, sb, da, db = cores[a["p"]], cores[b["p"]], cores[a["q"]], cores[b["q"]]
+            if topo.chip(da) == topo.chip(db) and topo.die(sa) == topo.die(sb):
+                c += max(0.0, min(a1, b1) - max(a0, b0))
+            if a["q"] == b["q"]:
+                c += max(0.0, 1.0 - abs(a1 - b1)) * min(a1, b1)
+    return c
+
+
+def _plan(dest, cores, topo):
+    orders = [_pieces(dest, p) for p in range(len(dest))]
+    for _ in range(6):
+        changed = False
+        for p in range(len(dest)):
+            best = min(_perms(orders[p]), key=lambda o: _cost(orders[:p] + [o] + orders[p + 1:], cores, topo))
+            if best != orders[p]:
+                orders[p], changed = best, True
+        if not changed:
+            break
+    for p, lst in enumerate(orders):
+        m = -1
+        for s in lst:
+            m &= topo.mask(cores[p], cores[s["q"]])
+        bits = [b for b in range(m.bit_length()) if (m >> b) & 1]
+        half = len(bits) // 2
+        last = len(lst) - 1
+        fuse = last % 2 == 1 and last > 1 and lst[-1]["n"] == lst[-2]["n"]
+        src, t = 0, 0.0
+        for k, s in enumerate(lst):
+            s["raw"] = k == 0 and s["n"] == 1
+            t += _dur(s["n"]) * (2 if s["raw"] else 1)
+            s["src"], s["when"], s["call"] = src, t, k
+            src += s["n"]
+            s["bits"] = bits[:half] if k % 2 == 0 else bits[half:]
+            if k == last and k % 2 == 0 and k > 0:
+                s["bits"] = bits
+            if fuse and k >= last - 1:
+                s["call"] = last - 1
+                s["when"] = t + (_dur(s["n"]) if k == last - 1 else 0.0)
+    return orders
+
+
+def _m(bits):
+    return sum(1 << b for b in bits)
 
 
 def _sender(g, core, T, topo, p, mine):
     S = T.sem
     hw = [g.sync, g.scalar]
-    g.sync.dma_start(T.wsb[:], T.w[:]).then_inc(S.ldw, 16)
+    w = T.wx[:, 0:TK]
+    g.sync.dma_start(w, T.w[:]).then_inc(S.ldw, 16)
     first = _runs(mine[0]["cs"])
     rest = _runs(sorted(c for s in mine[1:] for c in s["cs"]))
     sem_of_block = {}
     for i, (a, n) in enumerate(first + rest):
-        hw[(i + 1) % 2].dma_start(T.xsb[:, a * TK:(a + n) * TK], T.x[:, a * TK:(a + n) * TK]).then_inc(S["ldx%d" % i], 16)
+        into = T.wx[:, TK:2 * TK] if (i == 0 and mine[0]["raw"]) else T.xsb[:, a * TK:(a + n) * TK]
+        hw[(i + 1) % 2].dma_start(into, T.x[:, a * TK:(a + n) * TK]).then_inc(S["ldx%d" % i], 16)
         for c in range(a, a + n):
             sem_of_block[c] = i
     widest = max(s["n"] for s in mine) * TK
@@ -72,9 +140,19 @@ def _sender(g, core, T, topo, p, mine):
     g.vector.wait_ge(S.zr, 1)
     g.tensor.wait_ge(S.ldw, 16)
     seen = set()
-    mask = _mask_of(core, [T.cores[s["q"]] for s in mine], topo)
-    eng = bin(mask).count("1")
+    pending = []
     for k, s in enumerate(mine):
+        dst = T.cores[s["q"]]
+        assert topo.may_write(core, dst)
+        rid, pid, _ = topo.addr(dst)
+        arr = S["arr%d" % s["dst"]]
+        wd = s["n"] * TK
+        lo = s["dst"] * TK
+        if s["raw"]:
+            g.wait_ge(S.ldw, 16)
+            g.wait_ge(S["ldx%d" % sem_of_block[s["cs"][0]]], 16)
+            g.remote_dma(T.rl[:, p * 2 * TK:(p + 1) * 2 * TK], T.wx[:], arr, S.sent, pid, rid, _m(s["bits"]))
+            continue
         ps = T["ps%d" % k]
         runs = _runs(s["cs"])
         at = 0
@@ -84,34 +162,43 @@ def _sender(g, core, T, topo, p, mine):
                 if i not in seen:
                     seen.add(i)
                     g.tensor.wait_ge(S["ldx%d" % i], 16)
-            g.tensor.matmul(ps[:, at * TK:(at + n) * TK], T.wsb[:], T.xsb[:, a * TK:(a + n) * TK],
+            g.tensor.matmul(ps[:, at * TK:(at + n) * TK], w, T.xsb[:, a * TK:(a + n) * TK],
                             start=True, stop=True).then_inc(S["mm%d" % k], 1)
             at += n
-        wd = s["n"] * TK
         hcols = T.h[:, s["src"] * TK:s["src"] * TK + wd]
         g.vector.wait_ge(S["mm%d" % k], len(runs))
         g.vector.tensor_tensor(out=hcols, in0=ps[:, 0:wd], in1=T.zero[:, 0:wd], op=AluOpType.max).then_inc(S["ew%d" % k], 1)
-        dst = T.cores[s["q"]]
-        assert topo.may_write(core, dst)
-        rid, pid, _ = topo.addr(dst)
         g.wait_ge(S["ew%d" % k], 1)
-        g.remote_dma(T.land[:, s["dst"] * TK:s["dst"] * TK + wd], hcols, S["arr%d" % p], S.sent, pid, rid, mask)
-    g.wait_ge(S.sent, eng * len(mine))
+        pending.append(RemoteDMATransfer(dst_ids=[DstId(rid=rid, pnc=pid)], dma_engine_mask=_m(s["bits"]),
+                                         remote_sem=arr, src=hcols, dst=T.land[:, lo:lo + wd]))
+        if k + 1 == len(mine) or mine[k + 1]["call"] != s["call"]:
+            g.remote_dma_fused(pending, local_sem=S.sent)
+            pending = []
+    g.wait_ge(S.sent, sum(len(s["bits"]) for s in mine))
 
 
 def _receiver(g, core, T, topo, q, sends):
     S = T.sem
     hw = [g.scalar, g.sync]
-    g.sync.dma_start(T.wsb[:], T.w[:]).then_inc(S.ldw, 16)
+    w = T.wx[:, 0:TK]
+    g.sync.dma_start(w, T.w[:]).then_inc(S.ldw, 16)
+    g.vector.memset(T.zero[:, 0:TK], 0.0).then_inc(S.zr, 1)
+    g.vector.wait_ge(S.zr, 1)
     g.tensor.wait_ge(S.ldw, 16)
     mine = sorted((s for lst in sends for s in lst if s["q"] == q), key=lambda s: (s["when"], s["p"]))
     for k, s in enumerate(mine):
-        src = T.cores[s["p"]]
-        eng = bin(_mask_of(src, [T.cores[t["q"]] for t in sends[s["p"]]], topo)).count("1")
         lo, hi = s["dst"] * TK, (s["dst"] + s["n"]) * TK
         ps = T["ps%d" % k]
-        g.tensor.wait_ge(S["arr%d" % s["p"]], eng)
-        g.tensor.matmul(ps[:, 0:hi - lo], T.wsb[:], T.land[:, lo:hi], start=True, stop=True).then_inc(S["mm%d" % k], 1)
+        g.tensor.wait_ge(S["arr%d" % s["dst"]], len(s["bits"]))
+        if s["raw"]:
+            at = s["p"] * 2 * TK
+            g.tensor.matmul(ps[:, 0:TK], T.rl[:, at:at + TK], T.rl[:, at + TK:at + 2 * TK],
+                            start=True, stop=True).then_inc(S["rm%d" % k], 1)
+            g.vector.wait_ge(S["rm%d" % k], 1)
+            g.vector.tensor_tensor(out=T.land[:, lo:hi], in0=ps[:, 0:TK], in1=T.zero[:, 0:TK],
+                                   op=AluOpType.max).then_inc(S["re%d" % k], 1)
+            g.tensor.wait_ge(S["re%d" % k], 1)
+        g.tensor.matmul(ps[:, 0:hi - lo], w, T.land[:, lo:hi], start=True, stop=True).then_inc(S["mm%d" % k], 1)
         g.vector.wait_ge(S["mm%d" % k], 1)
         g.vector.tensor_copy(out=T.res[:, lo:hi], in_=ps[:, 0:hi - lo]).then_inc(S["ew%d" % k], 1)
         hw[k % 2].wait_ge(S["ew%d" % k], 1)
@@ -124,8 +211,9 @@ def rank_program(g, core, T, topo):
     rank = T.rank_of(core)
     if rank is None:
         return
-    sends = _plan(T.tables["DEST"])
-    if rank < len(sends):
+    dest = T.tables["DEST"]
+    sends = _plan(dest, T.cores, topo)
+    if rank < len(dest):
         _sender(g, core, T, topo, rank, sends[rank])
     else:
         _receiver(g, core, T, topo, rank, sends)

from concourse.mybir import dt, AluOpType
from concourse.bass import DstId, RemoteDMATransfer

NP, NBK, TK, CAP = 5, 4, 128, 6

SCRATCH = {
    "wx": ("sbuf", [128, 2 * TK], "bfloat16"),
    "xsb": ("sbuf", [128, NBK * TK], "bfloat16"),
    "zero": ("sbuf", [128, NBK * TK], "float32"),
    "h": ("sbuf", [128, NBK * TK], "bfloat16"),
    "land": ("sbuf", [128, CAP * TK], "bfloat16"),
    "rl": ("sbuf", [128, NP * 2 * TK], "bfloat16"),
    "res": ("sbuf", [128, CAP * TK], "bfloat16"),
}
for _i in range(CAP):
    SCRATCH["ps%d" % _i] = ("psum", [128, 512], "float32")

SEMAPHORES = (["ldw", "zr", "sent"]
              + ["ldx%d" % i for i in range(NBK)]
              + ["mm%d" % i for i in range(CAP)]
              + ["ew%d" % i for i in range(CAP)]
              + ["rm%d" % i for i in range(CAP)]
              + ["re%d" % i for i in range(CAP)]
              + ["arr%d" % i for i in range(CAP)]
              + ["st%d" % i for i in range(CAP)])


def _runs(cs):
    out = []
    for c in cs:
        if out and out[-1][0] + out[-1][1] == c:
            out[-1][1] += 1
        else:
            out.append([c, 1])
    return [(a, n) for a, n in out]


def _perms(lst):
    if len(lst) <= 1:
        return [list(lst)]
    return [[lst[i]] + r for i in range(len(lst)) for r in _perms(lst[:i] + lst[i + 1:])]


def _pieces(dest, p):
    byq = {}
    for c, q in enumerate(dest[p]):
        byq.setdefault(q, []).append(c)
    out = []
    for q in sorted(byq):
        cs = byq[q]
        at = sum(1 for pp in range(p) for qq in dest[pp] if qq == q)
        for part in ([cs] if len(cs) < 3 else [cs[:1], cs[1:]]):
            out.append({"p": p, "q": q, "cs": part, "n": len(part), "dst": at})
            at += len(part)
    return out


def _dur(n):
    return 1.0 + 0.3 * n


def _cost(orders, cores, topo):
    ev, c, load = [], 0.0, {}
    for lst in orders:
        t = 0.0
        c += 100 * (lst[0]["n"] - 1) + 100 * (lst[-1]["n"] - 1)
        for k, s in enumerate(lst):
            d = _dur(s["n"]) * (2 if k == 0 else 1)
            ev.append((t, t + d, s))
            t += d
            sc, dc = cores[s["p"]], cores[s["q"]]
            if topo.chip(sc) != topo.chip(dc):
                port = (topo.chip(dc), topo.die(sc))
                load[port] = load.get(port, 0) + s["n"] + (1 if k == 0 else 0)
    c += 10 * max(load.values())
    for i, (a0, a1, a) in enumerate(ev):
        for b0, b1, b in ev[:i]:
            if a["p"] == b["p"]:
                continue
            sa, sb, da, db = cores[a["p"]], cores[b["p"]], cores[a["q"]], cores[b["q"]]
            if topo.chip(da) == topo.chip(db) and topo.die(sa) == topo.die(sb):
                c += max(0.0, min(a1, b1) - max(a0, b0))
            if a["q"] == b["q"]:
                c += max(0.0, 1.0 - abs(a1 - b1)) * min(a1, b1)
    return c


def _plan(dest, cores, topo):
    orders = [_pieces(dest, p) for p in range(len(dest))]
    for _ in range(6):
        changed = False
        for p in range(len(dest)):
            best = min(_perms(orders[p]), key=lambda o: _cost(orders[:p] + [o] + orders[p + 1:], cores, topo))
            if best != orders[p]:
                orders[p], changed = best, True
        if not changed:
            break
    for p, lst in enumerate(orders):
        m = -1
        for s in lst:
            m &= topo.mask(cores[p], cores[s["q"]])
        bits = [b for b in range(m.bit_length()) if (m >> b) & 1]
        half = len(bits) // 2
        last = len(lst) - 1
        fuse = last % 2 == 1 and last > 1 and lst[-1]["n"] == lst[-2]["n"]
        src, t = 0, 0.0
        for k, s in enumerate(lst):
            s["raw"] = k == 0 and s["n"] == 1
            t += _dur(s["n"]) * (2 if s["raw"] else 1)
            s["src"], s["when"], s["call"] = src, t, k
            src += s["n"]
            s["bits"] = bits[:half] if k % 2 == 0 else bits[half:]
            if k == last and k % 2 == 0 and k > 0:
                s["bits"] = bits
            if fuse and k >= last - 1:
                s["call"] = last - 1
                s["when"] = t + (_dur(s["n"]) if k == last - 1 else 0.0)
    return orders


def _m(bits):
    return sum(1 << b for b in bits)


def _sender(g, core, T, topo, p, mine):
    S = T.sem
    hw = [g.sync, g.scalar]
    w = T.wx[:, 0:TK]
    g.sync.dma_start(w, T.w[:]).then_inc(S.ldw, 16)
    first = _runs(mine[0]["cs"])
    rest = _runs(sorted(c for s in mine[1:] for c in s["cs"]))
    sem_of_block = {}
    for i, (a, n) in enumerate(first + rest):
        into = T.wx[:, TK:2 * TK] if (i == 0 and mine[0]["raw"]) else T.xsb[:, a * TK:(a + n) * TK]
        hw[(i + 1) % 2].dma_start(into, T.x[:, a * TK:(a + n) * TK]).then_inc(S["ldx%d" % i], 16)
        for c in range(a, a + n):
            sem_of_block[c] = i
    widest = max(s["n"] for s in mine) * TK
    g.vector.memset(T.zero[:, 0:widest], 0.0).then_inc(S.zr, 1)
    g.vector.wait_ge(S.zr, 1)
    g.tensor.wait_ge(S.ldw, 16)
    seen = set()
    pending = []
    for k, s in enumerate(mine):
        dst = T.cores[s["q"]]
        assert topo.may_write(core, dst)
        rid, pid, _ = topo.addr(dst)
        arr = S["arr%d" % s["dst"]]
        wd = s["n"] * TK
        lo = s["dst"] * TK
        if s["raw"]:
            g.wait_ge(S.ldw, 16)
            g.wait_ge(S["ldx%d" % sem_of_block[s["cs"][0]]], 16)
            g.remote_dma(T.rl[:, p * 2 * TK:(p + 1) * 2 * TK], T.wx[:], arr, S.sent, pid, rid, _m(s["bits"]))
            continue
        ps = T["ps%d" % k]
        runs = _runs(s["cs"])
        at = 0
        for a, n in runs:
            for c in range(a, a + n):
                i = sem_of_block[c]
                if i not in seen:
                    seen.add(i)
                    g.tensor.wait_ge(S["ldx%d" % i], 16)
            g.tensor.matmul(ps[:, at * TK:(at + n) * TK], w, T.xsb[:, a * TK:(a + n) * TK],
                            start=True, stop=True).then_inc(S["mm%d" % k], 1)
            at += n
        hcols = T.h[:, s["src"] * TK:s["src"] * TK + wd]
        g.vector.wait_ge(S["mm%d" % k], len(runs))
        g.vector.tensor_tensor(out=hcols, in0=ps[:, 0:wd], in1=T.zero[:, 0:wd], op=AluOpType.max).then_inc(S["ew%d" % k], 1)
        g.wait_ge(S["ew%d" % k], 1)
        pending.append(RemoteDMATransfer(dst_ids=[DstId(rid=rid, pnc=pid)], dma_engine_mask=_m(s["bits"]),
                                         remote_sem=arr, src=hcols, dst=T.land[:, lo:lo + wd]))
        if k + 1 == len(mine) or mine[k + 1]["call"] != s["call"]:
            g.remote_dma_fused(pending, local_sem=S.sent)
            pending = []
    g.wait_ge(S.sent, sum(len(s["bits"]) for s in mine))


def _receiver(g, core, T, topo, q, sends):
    S = T.sem
    hw = [g.scalar, g.sync]
    w = T.wx[:, 0:TK]
    g.sync.dma_start(w, T.w[:]).then_inc(S.ldw, 16)
    g.vector.memset(T.zero[:, 0:TK], 0.0).then_inc(S.zr, 1)
    g.vector.wait_ge(S.zr, 1)
    g.tensor.wait_ge(S.ldw, 16)
    mine = sorted((s for lst in sends for s in lst if s["q"] == q), key=lambda s: (s["when"], s["p"]))
    for k, s in enumerate(mine):
        lo, hi = s["dst"] * TK, (s["dst"] + s["n"]) * TK
        ps = T["ps%d" % k]
        g.tensor.wait_ge(S["arr%d" % s["dst"]], len(s["bits"]))
        if s["raw"]:
            at = s["p"] * 2 * TK
            g.tensor.matmul(ps[:, 0:TK], T.rl[:, at:at + TK], T.rl[:, at + TK:at + 2 * TK],
                            start=True, stop=True).then_inc(S["rm%d" % k], 1)
            g.vector.wait_ge(S["rm%d" % k], 1)
            g.vector.tensor_tensor(out=T.land[:, lo:hi], in0=ps[:, 0:TK], in1=T.zero[:, 0:TK],
                                   op=AluOpType.max).then_inc(S["re%d" % k], 1)
            g.tensor.wait_ge(S["re%d" % k], 1)
        g.tensor.matmul(ps[:, 0:hi - lo], w, T.land[:, lo:hi], start=True, stop=True).then_inc(S["mm%d" % k], 1)
        g.vector.wait_ge(S["mm%d" % k], 1)
        g.vector.tensor_copy(out=T.res[:, lo:hi], in_=ps[:, 0:hi - lo]).then_inc(S["ew%d" % k], 1)
        hw[k % 2].wait_ge(S["ew%d" % k], 1)
        hw[k % 2].dma_start(T.y[:, lo:hi], T.res[:, lo:hi]).then_inc(S["st%d" % k], 16)
    for k in range(len(mine)):
        hw[k % 2].wait_ge(S["st%d" % k], 16)


def rank_program(g, core, T, topo):
    rank = T.rank_of(core)
    if rank is None:
        return
    dest = T.tables["DEST"]
    sends = _plan(dest, T.cores, topo)
    if rank < len(dest):
        _sender(g, core, T, topo, rank, sends[rank])
    else:
        _receiver(g, core, T, topo, rank, sends)
